import numpy as np, ml_dtypes
CORES = [6,10,22,26,38,42,54,58]
N = 8
def setup_inputs(rng):
    return {"x": rng.standard_normal((N, 128, 512), dtype=np.float32).astype(ml_dtypes.bfloat16)}
def reference(x):
    s = x.min(axis=0)
    return {"y": np.broadcast_to(s, (N,) + s.shape)}

@@ -1,0 +1,74 @@
+from concourse.bass import DstId, RemoteDMATransfer
+
+NR = 8
+ROWS, COLS = 128, 512
+PARTS = 1
+HELP_XOR = [1]
+W = COLS // (NR * PARTS)
+
+SCRATCH = {
+    "xs": ("dram", [PARTS * NR, 128, W], "bfloat16"),
+    "gat": ("dram", [NR, 128, W], "bfloat16"),
+    "res": ("dram", [PARTS * NR, 128, W], "bfloat16"),
+}
+SEMAPHORES = (["ld%d" % p for p in range(PARTS)] + ["arr%d" % p for p in range(PARTS)]
+              + ["st%d" % p for p in range(PARTS)] + ["got", "sent"])
+
+OFF_ALL = 0x00FF
+ON_HI = 0xFF00
+
+
+def _dst(topo, c):
+    rid, pid, _se = topo.addr(c)
+    return DstId(rid=rid, pnc=pid)
+
+
+def rank_program(g, core, T, topo):
+    cores = list(T.cores)
+    rank = T.rank_of(core)
+
+    if rank is not None:
+        queues = [g.sync, g.scalar]
+        rp = ROWS // PARTS
+        for p in range(PARTS):
+            q = queues[p % 2]
+            q.dma_start(T.xs[p * NR:(p + 1) * NR], T.x[p * rp:(p + 1) * rp, :]).then_inc(T.sem["ld%d" % p], 16)
+        for p in range(PARTS):
+            q = queues[p % 2]
+            q.wait_ge(T.sem["arr%d" % p], NR * 8)
+            q.dma_start(T.y[p * rp:(p + 1) * rp, :], T.res[p * NR:(p + 1) * NR]).then_inc(T.sem["st%d" % p], 16)
+        sent = 0
+        for p in range(PARTS):
+            g.wait_ge(T.sem["ld%d" % p], 16)
+            trs = []
+            eng = 0
+            for j in range(NR):
+                h = cores[j] ^ HELP_XOR[p]
+                if j == rank:
+                    m = ON_HI
+                    sent += 8
+                else:
+                    m = 1 << eng
+                    eng += 1
+                    sent += 1
+                trs.append(RemoteDMATransfer(dst_ids=[_dst(topo, h)], dma_engine_mask=m, remote_sem=T.sem.got,
+                                             src=T.xs[p * NR + j], dst=T.gat[rank], alu_op=0))
+            g.remote_dma_fused(trs, local_sem=T.sem.sent)
+        g.wait_ge(T.sem.sent, sent)
+        for p in range(PARTS):
+            g.wait_ge(T.sem["st%d" % p], 16)
+        return
+
+    for p in range(PARTS):
+        owner = core ^ HELP_XOR[p]
+        j = T.rank_of(owner)
+        if j is None:
+            continue
+        g.wait_ge(T.sem.got, 7 + 8)
+        tr = RemoteDMATransfer(dst_ids=[_dst(topo, c) for c in cores], dma_engine_mask=OFF_ALL,
+                               remote_sem=T.sem["arr%d" % p],
+                               srcs=[T.gat[r] for r in range(NR)],
+                               dsts=[T.res[p * NR + j] for _c in cores], alu_op=3)
+        g.remote_dma_fused([tr], local_sem=T.sem.sent)
+        g.wait_ge(T.sem.sent, 8)
+        return

@@ -2,8 +2,8 @@ from concourse.bass import DstId, RemoteDMATransfer
 
 NR = 8
 ROWS, COLS = 128, 512
-PARTS = 1
-HELP_XOR = [1]
+PARTS = 2
+HELP_XOR = [4, 1]
 W = COLS // (NR * PARTS)
 
 SCRATCH = {

@@ -2,15 +2,15 @@ from concourse.bass import DstId, RemoteDMATransfer
 
 NR = 8
 ROWS, COLS = 128, 512
-PARTS = 2
-HELP_XOR = [4, 1]
-W = COLS // (NR * PARTS)
+WS = [28, 20, 16]
+HELP_XOR = [4, 5, 1]
+PARTS = len(WS)
 
-SCRATCH = {
-    "xs": ("dram", [PARTS * NR, 128, W], "bfloat16"),
-    "gat": ("dram", [NR, 128, W], "bfloat16"),
-    "res": ("dram", [PARTS * NR, 128, W], "bfloat16"),
-}
+SCRATCH = {}
+for _p in range(PARTS):
+    SCRATCH["xs%d" % _p] = ("dram", [NR, 128, WS[_p]], "bfloat16")
+    SCRATCH["gat%d" % _p] = ("dram", [NR, 128, WS[_p]], "bfloat16")
+    SCRATCH["res%d" % _p] = ("dram", [NR, 128, WS[_p]], "bfloat16")
 SEMAPHORES = (["ld%d" % p for p in range(PARTS)] + ["arr%d" % p for p in range(PARTS)]
               + ["st%d" % p for p in range(PARTS)] + ["got", "sent"])
 
@@ -23,26 +23,36 @@ def _dst(topo, c):
     return DstId(rid=rid, pnc=pid)
 
 
+def _hops(topo, a, b):
+    ca, cb = topo.chip(a), topo.chip(b)
+    if ca == cb:
+        return 0
+    if topo.mates(ca, cb) or topo.same_plane(ca, cb):
+        return 1
+    return 2
+
+
 def rank_program(g, core, T, topo):
     cores = list(T.cores)
     rank = T.rank_of(core)
 
     if rank is not None:
         queues = [g.sync, g.scalar]
-        rp = ROWS // PARTS
+        row0 = [2 * sum(WS[:p]) for p in range(PARTS + 1)]
         for p in range(PARTS):
             q = queues[p % 2]
-            q.dma_start(T.xs[p * NR:(p + 1) * NR], T.x[p * rp:(p + 1) * rp, :]).then_inc(T.sem["ld%d" % p], 16)
+            q.dma_start(T["xs%d" % p][:], T.x[row0[p]:row0[p + 1], :]).then_inc(T.sem["ld%d" % p], 16)
         for p in range(PARTS):
             q = queues[p % 2]
             q.wait_ge(T.sem["arr%d" % p], NR * 8)
-            q.dma_start(T.y[p * rp:(p + 1) * rp, :], T.res[p * NR:(p + 1) * NR]).then_inc(T.sem["st%d" % p], 16)
+            q.dma_start(T.y[row0[p]:row0[p + 1], :], T["res%d" % p][:]).then_inc(T.sem["st%d" % p], 16)
+        order = sorted(range(NR), key=lambda j: -_hops(topo, core, cores[j]))
         sent = 0
         for p in range(PARTS):
             g.wait_ge(T.sem["ld%d" % p], 16)
             trs = []
             eng = 0
-            for j in range(NR):
+            for j in order:
                 h = cores[j] ^ HELP_XOR[p]
                 if j == rank:
                     m = ON_HI
@@ -52,7 +62,7 @@ def rank_program(g, core, T, topo):
                     eng += 1
                     sent += 1
                 trs.append(RemoteDMATransfer(dst_ids=[_dst(topo, h)], dma_engine_mask=m, remote_sem=T.sem.got,
-                                             src=T.xs[p * NR + j], dst=T.gat[rank], alu_op=0))
+                                             src=T["xs%d" % p][j], dst=T["gat%d" % p][rank], alu_op=0))
             g.remote_dma_fused(trs, local_sem=T.sem.sent)
         g.wait_ge(T.sem.sent, sent)
         for p in range(PARTS):
@@ -65,10 +75,11 @@ def rank_program(g, core, T, topo):
         if j is None:
             continue
         g.wait_ge(T.sem.got, 7 + 8)
-        tr = RemoteDMATransfer(dst_ids=[_dst(topo, c) for c in cores], dma_engine_mask=OFF_ALL,
+        order = sorted(range(NR), key=lambda k: -_hops(topo, core, cores[k]))
+        tr = RemoteDMATransfer(dst_ids=[_dst(topo, cores[k]) for k in order], dma_engine_mask=OFF_ALL,
                                remote_sem=T.sem["arr%d" % p],
-                               srcs=[T.gat[r] for r in range(NR)],
-                               dsts=[T.res[p * NR + j] for _c in cores], alu_op=3)
+                               srcs=[T["gat%d" % p][r] for r in range(NR)],
+                               dsts=[T["res%d" % p][j] for _k in order], alu_op=3)
         g.remote_dma_fused([tr], local_sem=T.sem.sent)
         g.wait_ge(T.sem.sent, 8)
         return

from concourse.bass import DstId, RemoteDMATransfer

NR = 8
ROWS, COLS = 128, 512
WS = [28, 20, 16]
HELP_XOR = [4, 5, 1]
PARTS = len(WS)

SCRATCH = {}
for _p in range(PARTS):
    SCRATCH["xs%d" % _p] = ("dram", [NR, 128, WS[_p]], "bfloat16")
    SCRATCH["gat%d" % _p] = ("dram", [NR, 128, WS[_p]], "bfloat16")
    SCRATCH["res%d" % _p] = ("dram", [NR, 128, WS[_p]], "bfloat16")
SEMAPHORES = (["ld%d" % p for p in range(PARTS)] + ["arr%d" % p for p in range(PARTS)]
              + ["st%d" % p for p in range(PARTS)] + ["got", "sent"])

OFF_ALL = 0x00FF
ON_HI = 0xFF00


def _dst(topo, c):
    rid, pid, _se = topo.addr(c)
    return DstId(rid=rid, pnc=pid)


def _hops(topo, a, b):
    ca, cb = topo.chip(a), topo.chip(b)
    if ca == cb:
        return 0
    if topo.mates(ca, cb) or topo.same_plane(ca, cb):
        return 1
    return 2


def rank_program(g, core, T, topo):
    cores = list(T.cores)
    rank = T.rank_of(core)

    if rank is not None:
        queues = [g.sync, g.scalar]
        row0 = [2 * sum(WS[:p]) for p in range(PARTS + 1)]
        for p in range(PARTS):
            q = queues[p % 2]
            q.dma_start(T["xs%d" % p][:], T.x[row0[p]:row0[p + 1], :]).then_inc(T.sem["ld%d" % p], 16)
        for p in range(PARTS):
            q = queues[p % 2]
            q.wait_ge(T.sem["arr%d" % p], NR * 8)
            q.dma_start(T.y[row0[p]:row0[p + 1], :], T["res%d" % p][:]).then_inc(T.sem["st%d" % p], 16)
        order = sorted(range(NR), key=lambda j: -_hops(topo, core, cores[j]))
        sent = 0
        for p in range(PARTS):
            g.wait_ge(T.sem["ld%d" % p], 16)
            trs = []
            eng = 0
            for j in order:
                h = cores[j] ^ HELP_XOR[p]
                if j == rank:
                    m = ON_HI
                    sent += 8
                else:
                    m = 1 << eng
                    eng += 1
                    sent += 1
                trs.append(RemoteDMATransfer(dst_ids=[_dst(topo, h)], dma_engine_mask=m, remote_sem=T.sem.got,
                                             src=T["xs%d" % p][j], dst=T["gat%d" % p][rank], alu_op=0))
            g.remote_dma_fused(trs, local_sem=T.sem.sent)
        g.wait_ge(T.sem.sent, sent)
        for p in range(PARTS):
            g.wait_ge(T.sem["st%d" % p], 16)
        return

    for p in range(PARTS):
        owner = core ^ HELP_XOR[p]
        j = T.rank_of(owner)
        if j is None:
            continue
        g.wait_ge(T.sem.got, 7 + 8)
        order = sorted(range(NR), key=lambda k: -_hops(topo, core, cores[k]))
        tr = RemoteDMATransfer(dst_ids=[_dst(topo, cores[k]) for k in order], dma_engine_mask=OFF_ALL,
                               remote_sem=T.sem["arr%d" % p],
                               srcs=[T["gat%d" % p][r] for r in range(NR)],
                               dsts=[T["res%d" % p][j] for _k in order], alu_op=3)
        g.remote_dma_fused([tr], local_sem=T.sem.sent)
        g.wait_ge(T.sem.sent, 8)
        return
